import numpy as np, ml_dtypes
CORES = [3,7,11,15,131,135,139,143]
N = 8
import mx_ref
NC, WT = 128, 1
LR = np.float32(2.0 ** -3)
BF = ml_dtypes.bfloat16
def cut(t, i, w=512):
    return t[:, w * i:w * i + w]
def setup_inputs(rng):
    def f(*shape):
        return mx_ref.flush((rng.standard_normal(shape, dtype=np.float32) * np.exp2(rng.integers(-2, 3, shape[:-1] + (1,)))).astype(BF))
    return {"w": f(N, 128, WT * 512), "gr": f(N, 128, WT * 512), "x": f(N, 128, 4 * NC)}
def setup_inputs_blocks(rng):
    d = setup_inputs(rng)
    for k in ("x",): d[k] = mx_ref.spread(d[k], rng, 4)
    for k in ("w", "gr"): d[k] = mx_ref.spread(d[k], rng, 2)
    return d
def setup_inputs_wide(rng):
    d = setup_inputs(rng)
    for k in ("w", "gr", "x"): d[k] = mx_ref.flush((d[k].astype(np.float32) * np.exp2(rng.integers(-4, 5, (N, 1, 1))).astype(np.float32)).astype(BF))
    return d
def setup_inputs_faint(rng):
    d = setup_inputs(rng); d["gr"] = mx_ref.flush((d["gr"].astype(np.float32) * np.float32(2.0 ** -12)).astype(BF))
    return d
def reference(w, gr, x):
    H = [mx_ref.quantize((cut(w[j], i).astype(np.float32) - cut(gr[j], i).astype(np.float32) * LR).astype(BF)) for j in range(N) for i in range(WT)]
    y = np.zeros((N, 128, N * WT * NC), np.float32)
    for r in range(N):
        X = mx_ref.quantize(x[r])
        for b in range(N * WT):
            y[r][:, NC * b:NC * b + NC] = mx_ref.matmul(H[b], X)
    return {"y": y}

@@ -1,0 +1,145 @@
+from concourse.bass import DstId, RemoteDMATransfer
+from concourse.mybir import dt, AluOpType, ActivationFunctionType
+
+N = 8
+NC = 128
+OWN, PLANE, DIAG, MATE_S, MATE_O, SIB, SIB_PLANE, SIB_DIAG = range(N)
+
+SCRATCH = {
+    "wb": ("sbuf", [128, 4 * NC], "bfloat16"),
+    "gb": ("sbuf", [128, 4 * NC], "bfloat16"),
+    "xb": ("sbuf", [128, 4 * NC], "bfloat16"),
+    "step": ("sbuf", [128, 4 * NC], "bfloat16"),
+    "vb": ("sbuf", [128, 4 * NC], "bfloat16"),
+    "codes": ("sbuf", [128, N * NC], "float8_e4m3fn_x4"),
+    "planes": ("sbuf", [128, N * NC], "uint8"),
+    "xq": ("sbuf", [128, NC], "float8_e4m3fn_x4"),
+    "xs": ("sbuf", [128, NC], "uint8"),
+    "ps": ("psum", [128, 512 * N], "float32"),
+    "yb": ("sbuf", [128, N * NC], "float32"),
+}
+SEMAPHORES = (["ld_g", "ld_w", "ld_x", "stepped", "made", "vq", "xqd", "sent", "far", "mate", "sib", "fwd",
+               "st_a", "st_b", "st_c", "st_d", "st_e", "st_f"]
+              + ["mm%d" % s for s in range(N)] + ["cp%d" % s for s in range(N)])
+
+
+def _roles(core, T, topo):
+    out = {OWN: core}
+    for c in T.cores:
+        if c == core:
+            continue
+        near = topo.die(c) == topo.die(core)
+        if topo.host(c) == topo.host(core) and topo.chip(c) == topo.chip(core):
+            out[SIB] = c
+        elif topo.mates(core, c):
+            out[MATE_S if near else MATE_O] = c
+        elif near:
+            out[PLANE if topo.same_plane(core, c) else DIAG] = c
+    return out
+
+
+def rank_program(g, core, T, topo):
+    rank = T.rank_of(core)
+    if rank is None:
+        return
+    S = T.sem
+    role = _roles(core, T, topo)
+    sib = role[SIB]
+    sib_role = _roles(sib, T, topo)
+    owner = dict(role)
+    owner[SIB_PLANE] = sib_role[PLANE]
+    owner[SIB_DIAG] = sib_role[DIAG]
+
+    def codes(s, k=1):
+        return T.codes[:, NC * s:NC * (s + k)]
+
+    def planes(s, k=1):
+        return T.planes[:, NC * s:NC * (s + k)]
+
+    def raw(s, k=1):
+        return codes(s, k).bitcast(dt.uint8)
+
+    g.sync.dma_start(T.gb[:], T.gr[:]).then_inc(S.ld_g, 16)
+    g.scalar.dma_start(T.wb[:], T.w[:]).then_inc(S.ld_w, 16)
+    g.sync.wait_ge(S.ld_g, 16)
+    g.sync.dma_start(T.xb[:], T.x[:]).then_inc(S.ld_x, 16)
+
+    g.vector.wait_ge(S.ld_g, 16)
+    g.vector.tensor_scalar(T.step[:], T.gb[:], 0.125, None, AluOpType.mult).then_inc(S.stepped, 1)
+    g.vector.wait_ge(S.ld_w, 16)
+    g.vector.wait_ge(S.stepped, 1)
+    g.vector.tensor_tensor(T.vb[:], T.wb[:], T.step[:], AluOpType.subtract).then_inc(S.made, 1)
+    g.vector.wait_ge(S.made, 1)
+    g.vector.quantize_mx(codes(OWN), planes(OWN), T.vb[:]).then_inc(S.vq, 1)
+    g.vector.wait_ge(S.ld_x, 16)
+    g.vector.quantize_mx(T.xq[:], T.xs[:], T.xb[:]).then_inc(S.xqd, 1)
+
+    off = topo.mask(core, role[PLANE])
+    on = topo.mask(core, sib) & ~off
+
+    def to(d):
+        rid, pid = topo.addr(d, core)
+        return DstId(rid=rid, pnc=pid)
+
+    def own_to(view, roles, mask, sem):
+        return RemoteDMATransfer(dst_ids=[to(role[r]) for r in roles], dma_engine_mask=mask, remote_sem=sem,
+                                 srcs=[view(OWN)], dsts=[view(r) for r in roles])
+
+    g.wait_ge(S.vq, 1)
+    for view in (raw, planes):
+        g.remote_dma_fused([own_to(view, (DIAG, PLANE), off, S.far)], local_sem=S.sent)
+    for view in (raw, planes):
+        g.remote_dma_fused([own_to(view, (MATE_S, MATE_O), off, S.mate), own_to(view, (SIB,), on, S.sib)], local_sem=S.sent)
+    e_off, e_on = bin(off).count("1"), bin(on).count("1")
+    g.wait_ge(S.far, 4 * e_off)
+    rid, pid = topo.addr(sib, core)
+    for view in (raw, planes):
+        g.remote_dma(view(SIB_PLANE, 2), view(PLANE, 2), S.fwd, S.sent, pid, rid, on)
+    g.wait_ge(S.sent, 4 * e_off + 4 * e_on)
+
+    def product(s):
+        g.tensor.matmul_mx(T.ps[:, 512 * s:512 * s + NC], codes(s), planes(s), T.xq[:], T.xs[:], True, True).then_inc(S["mm%d" % s], 1)
+
+    g.tensor.wait_ge(S.vq, 1)
+    g.tensor.wait_ge(S.xqd, 1)
+    product(OWN)
+    g.tensor.wait_ge(S.far, 4 * e_off)
+    product(PLANE)
+    product(DIAG)
+    g.tensor.wait_ge(S.sib, 2 * e_on)
+    product(SIB)
+    g.tensor.wait_ge(S.mate, 4 * e_off)
+    product(MATE_S)
+    product(MATE_O)
+    g.tensor.wait_ge(S.fwd, 2 * e_on)
+    product(SIB_PLANE)
+    product(SIB_DIAG)
+
+    def block(s):
+        j = T.rank_of(owner[s])
+        return NC * j, NC * (j + 1)
+
+    for s in (OWN, PLANE, MATE_S, SIB_PLANE):
+        a, b = block(s)
+        g.vector.wait_ge(S["mm%d" % s], 1)
+        g.vector.tensor_copy(T.yb[:, a:b], T.ps[:, 512 * s:512 * s + NC]).then_inc(S["cp%d" % s], 1)
+    for s in (DIAG, SIB, MATE_O, SIB_DIAG):
+        a, b = block(s)
+        g.scalar.wait_ge(S["mm%d" % s], 1)
+        g.scalar.activation(T.yb[:, a:b], T.ps[:, 512 * s:512 * s + NC], ActivationFunctionType.Copy).then_inc(S["cp%d" % s], 1)
+
+    def store(q, slots, sem):
+        for s in slots:
+            q.wait_ge(S["cp%d" % s], 1)
+        a, b = min(block(s)[0] for s in slots), max(block(s)[1] for s in slots)
+        q.dma_start(T.y[:, a:b], T.yb[:, a:b]).then_inc(sem, 16)
+
+    store(g.sync, (PLANE,), S.st_b)
+    store(g.sync, (DIAG,), S.st_c)
+    store(g.sync, (OWN, SIB), S.st_a)
+    store(g.sync, (MATE_S, MATE_O), S.st_d)
+    store(g.sync, (SIB_PLANE,), S.st_e)
+    store(g.scalar, (SIB_DIAG,), S.st_f)
+    for sem in (S.st_a, S.st_b, S.st_c, S.st_d, S.st_e):
+        g.sync.wait_ge(sem, 16)
+    g.scalar.wait_ge(S.st_f, 16)

@@ -3,7 +3,7 @@ from concourse.mybir import dt, AluOpType, ActivationFunctionType
 
 N = 8
 NC = 128
-OWN, PLANE, DIAG, MATE_S, MATE_O, SIB, SIB_PLANE, SIB_DIAG = range(N)
+OWN, SIB, MATE_S, MATE_O, PLANE, DIAG, SIB_PLANE, SIB_DIAG = range(N)
 
 SCRATCH = {
     "wb": ("sbuf", [128, 4 * NC], "bfloat16"),
@@ -18,7 +18,8 @@ SCRATCH = {
     "ps": ("psum", [128, 512 * N], "float32"),
     "yb": ("sbuf", [128, N * NC], "float32"),
 }
-SEMAPHORES = (["ld_g", "ld_w", "ld_x", "stepped", "made", "vq", "xqd", "sent", "far", "mate", "sib", "fwd",
+SEMAPHORES = (["ld_g", "ld_w0", "ld_w1", "ld_x", "stepped0", "stepped1", "made0", "made1", "vq", "xqd", "sent",
+               "far_p", "diag", "plane", "mate", "mate_p", "sib", "sib_p", "fwd_p", "fwd_d", "fwd_c",
                "st_a", "st_b", "st_c", "st_d", "st_e", "st_f"]
               + ["mm%d" % s for s in range(N)] + ["cp%d" % s for s in range(N)])
 
@@ -50,32 +51,40 @@ def rank_program(g, core, T, topo):
     owner[SIB_PLANE] = sib_role[PLANE]
     owner[SIB_DIAG] = sib_role[DIAG]
 
-    def codes(s, k=1):
-        return T.codes[:, NC * s:NC * (s + k)]
+    def codes(s):
+        return T.codes[:, NC * s:NC * (s + 1)]
 
     def planes(s, k=1):
         return T.planes[:, NC * s:NC * (s + k)]
 
-    def raw(s, k=1):
-        return codes(s, k).bitcast(dt.uint8)
+    def raw(s):
+        return codes(s).bitcast(dt.uint8)
 
+    H = 2 * NC
     g.sync.dma_start(T.gb[:], T.gr[:]).then_inc(S.ld_g, 16)
-    g.scalar.dma_start(T.wb[:], T.w[:]).then_inc(S.ld_w, 16)
+    for h in range(2):
+        g.scalar.dma_start(T.wb[:, H * h:H * (h + 1)], T.w[:, H * h:H * (h + 1)]).then_inc(S["ld_w%d" % h], 16)
     g.sync.wait_ge(S.ld_g, 16)
     g.sync.dma_start(T.xb[:], T.x[:]).then_inc(S.ld_x, 16)
 
     g.vector.wait_ge(S.ld_g, 16)
-    g.vector.tensor_scalar(T.step[:], T.gb[:], 0.125, None, AluOpType.mult).then_inc(S.stepped, 1)
-    g.vector.wait_ge(S.ld_w, 16)
-    g.vector.wait_ge(S.stepped, 1)
-    g.vector.tensor_tensor(T.vb[:], T.wb[:], T.step[:], AluOpType.subtract).then_inc(S.made, 1)
-    g.vector.wait_ge(S.made, 1)
+    g.vector.tensor_scalar(T.step[:, 0:H], T.gb[:, 0:H], 0.125, None, AluOpType.mult).then_inc(S.stepped0, 1)
+    g.scalar.wait_ge(S.ld_g, 16)
+    g.scalar.activation(T.step[:, H:2 * H], T.gb[:, H:2 * H], ActivationFunctionType.Copy, scale=0.125).then_inc(S.stepped1, 1)
+    for h in range(2):
+        g.vector.wait_ge(S["ld_w%d" % h], 16)
+        g.vector.wait_ge(S["stepped%d" % h], 1)
+        half = slice(H * h, H * (h + 1))
+        g.vector.tensor_tensor(T.vb[:, half], T.wb[:, half], T.step[:, half], AluOpType.subtract).then_inc(S["made%d" % h], 1)
+    g.vector.wait_ge(S.made0, 1)
+    g.vector.wait_ge(S.made1, 1)
     g.vector.quantize_mx(codes(OWN), planes(OWN), T.vb[:]).then_inc(S.vq, 1)
     g.vector.wait_ge(S.ld_x, 16)
     g.vector.quantize_mx(T.xq[:], T.xs[:], T.xb[:]).then_inc(S.xqd, 1)
 
     off = topo.mask(core, role[PLANE])
     on = topo.mask(core, sib) & ~off
+    e_off, e_on = bin(off).count("1"), bin(on).count("1")
 
     def to(d):
         rid, pid = topo.addr(d, core)
@@ -85,17 +94,23 @@ def rank_program(g, core, T, topo):
         return RemoteDMATransfer(dst_ids=[to(role[r]) for r in roles], dma_engine_mask=mask, remote_sem=sem,
                                  srcs=[view(OWN)], dsts=[view(r) for r in roles])
 
-    g.wait_ge(S.vq, 1)
-    for view in (raw, planes):
-        g.remote_dma_fused([own_to(view, (DIAG, PLANE), off, S.far)], local_sem=S.sent)
-    for view in (raw, planes):
-        g.remote_dma_fused([own_to(view, (MATE_S, MATE_O), off, S.mate), own_to(view, (SIB,), on, S.sib)], local_sem=S.sent)
-    e_off, e_on = bin(off).count("1"), bin(on).count("1")
-    g.wait_ge(S.far, 4 * e_off)
     rid, pid = topo.addr(sib, core)
-    for view in (raw, planes):
-        g.remote_dma(view(SIB_PLANE, 2), view(PLANE, 2), S.fwd, S.sent, pid, rid, on)
-    g.wait_ge(S.sent, 4 * e_off + 4 * e_on)
+    mrid, mpid = topo.addr(role[MATE_S], core)
+    g.wait_ge(S.vq, 1)
+    g.remote_dma_fused([own_to(planes, (DIAG, PLANE), off, S.far_p)], local_sem=S.sent)
+    g.remote_dma_fused([own_to(raw, (DIAG,), off, S.diag)], local_sem=S.sent)
+    g.remote_dma(planes(SIB), planes(OWN), S.sib_p, S.sent, pid, rid, on)
+    g.remote_dma_fused([own_to(raw, (PLANE,), off, S.plane), own_to(raw, (SIB,), on, S.sib)], local_sem=S.sent)
+    g.remote_dma_fused([own_to(raw, (MATE_S, MATE_O), off, S.mate)], local_sem=S.sent)
+    g.wait_ge(S.sib_p, e_on)
+    g.remote_dma(planes(MATE_S, 2), planes(OWN, 2), S.mate_p, S.sent, mpid, mrid, off)
+    g.wait_ge(S.far_p, 2 * e_off)
+    g.remote_dma(planes(SIB_PLANE, 2), planes(PLANE, 2), S.fwd_p, S.sent, pid, rid, on)
+    g.wait_ge(S.diag, e_off)
+    g.remote_dma(raw(SIB_DIAG), raw(DIAG), S.fwd_d, S.sent, pid, rid, on)
+    g.wait_ge(S.plane, e_off)
+    g.remote_dma(raw(SIB_PLANE), raw(PLANE), S.fwd_c, S.sent, pid, rid, on)
+    g.wait_ge(S.sent, 5 * e_off + 5 * e_on)
 
     def product(s):
         g.tensor.matmul_mx(T.ps[:, 512 * s:512 * s + NC], codes(s), planes(s), T.xq[:], T.xs[:], True, True).then_inc(S["mm%d" % s], 1)
@@ -103,27 +118,33 @@ def rank_program(g, core, T, topo):
     g.tensor.wait_ge(S.vq, 1)
     g.tensor.wait_ge(S.xqd, 1)
     product(OWN)
-    g.tensor.wait_ge(S.far, 4 * e_off)
-    product(PLANE)
+    g.tensor.wait_ge(S.far_p, 2 * e_off)
+    g.tensor.wait_ge(S.diag, e_off)
     product(DIAG)
-    g.tensor.wait_ge(S.sib, 2 * e_on)
+    g.tensor.wait_ge(S.sib, e_on)
+    g.tensor.wait_ge(S.sib_p, e_on)
     product(SIB)
-    g.tensor.wait_ge(S.mate, 4 * e_off)
+    g.tensor.wait_ge(S.plane, e_off)
+    product(PLANE)
+    g.tensor.wait_ge(S.fwd_p, e_on)
+    g.tensor.wait_ge(S.fwd_d, e_on)
+    product(SIB_DIAG)
+    g.tensor.wait_ge(S.mate_p, e_off)
+    g.tensor.wait_ge(S.mate, 2 * e_off)
     product(MATE_S)
     product(MATE_O)
-    g.tensor.wait_ge(S.fwd, 2 * e_on)
+    g.tensor.wait_ge(S.fwd_c, e_on)
     product(SIB_PLANE)
-    product(SIB_DIAG)
 
     def block(s):
         j = T.rank_of(owner[s])
         return NC * j, NC * (j + 1)
 
-    for s in (OWN, PLANE, MATE_S, SIB_PLANE):
+    for s in (OWN, SIB, SIB_DIAG, MATE_O):
         a, b = block(s)
         g.vector.wait_ge(S["mm%d" % s], 1)
         g.vector.tensor_copy(T.yb[:, a:b], T.ps[:, 512 * s:512 * s + NC]).then_inc(S["cp%d" % s], 1)
-    for s in (DIAG, SIB, MATE_O, SIB_DIAG):
+    for s in (DIAG, PLANE, MATE_S, SIB_PLANE):
         a, b = block(s)
         g.scalar.wait_ge(S["mm%d" % s], 1)
         g.scalar.activation(T.yb[:, a:b], T.ps[:, 512 * s:512 * s + NC], ActivationFunctionType.Copy).then_inc(S["cp%d" % s], 1)
@@ -134,12 +155,12 @@ def rank_program(g, core, T, topo):
         a, b = min(block(s)[0] for s in slots), max(block(s)[1] for s in slots)
         q.dma_start(T.y[:, a:b], T.yb[:, a:b]).then_inc(sem, 16)
 
-    store(g.sync, (PLANE,), S.st_b)
     store(g.sync, (DIAG,), S.st_c)
     store(g.sync, (OWN, SIB), S.st_a)
+    store(g.sync, (PLANE,), S.st_b)
+    store(g.sync, (SIB_DIAG,), S.st_e)
     store(g.sync, (MATE_S, MATE_O), S.st_d)
-    store(g.sync, (SIB_PLANE,), S.st_e)
-    store(g.scalar, (SIB_DIAG,), S.st_f)
+    store(g.scalar, (SIB_PLANE,), S.st_f)
     for sem in (S.st_a, S.st_b, S.st_c, S.st_d, S.st_e):
         g.sync.wait_ge(sem, 16)
     g.scalar.wait_ge(S.st_f, 16)

@@ -2,25 +2,29 @@ from concourse.bass import DstId, RemoteDMATransfer
 from concourse.mybir import dt, AluOpType, ActivationFunctionType
 
 N = 8
+WORLD = 256
 NC = 128
+EC = 32
 OWN, SIB, MATE_S, MATE_O, PLANE, DIAG, SIB_PLANE, SIB_DIAG = range(N)
+AT = [NC - EC, 2 * NC, 3 * NC, 4 * NC + EC] + [EC + NC * k for k in range(5, 9)]
+COLS = AT[SIB_DIAG] + NC
 
 SCRATCH = {
     "wb": ("sbuf", [128, 4 * NC], "bfloat16"),
     "gb": ("sbuf", [128, 4 * NC], "bfloat16"),
     "xb": ("sbuf", [128, 4 * NC], "bfloat16"),
     "step": ("sbuf", [128, 4 * NC], "bfloat16"),
-    "vb": ("sbuf", [128, 4 * NC], "bfloat16"),
-    "codes": ("sbuf", [128, N * NC], "float8_e4m3fn_x4"),
-    "planes": ("sbuf", [128, N * NC], "uint8"),
+    "vb": ("sbuf", [128, 8 * NC], "bfloat16"),
+    "codes": ("sbuf", [128, COLS], "float8_e4m3fn_x4"),
+    "planes": ("sbuf", [128, COLS], "uint8"),
     "xq": ("sbuf", [128, NC], "float8_e4m3fn_x4"),
     "xs": ("sbuf", [128, NC], "uint8"),
     "ps": ("psum", [128, 512 * N], "float32"),
     "yb": ("sbuf", [128, N * NC], "float32"),
 }
-SEMAPHORES = (["ld_g", "ld_w0", "ld_w1", "ld_x", "stepped0", "stepped1", "made0", "made1", "vq", "xqd", "sent",
-               "far_p", "diag", "plane", "mate", "mate_p", "sib", "sib_p", "fwd_p", "fwd_d", "fwd_c",
-               "st_a", "st_b", "st_c", "st_d", "st_e", "st_f"]
+SEMAPHORES = (["ld_g0", "ld_g1", "ld_w0", "ld_w1", "ld_w2", "ld_x", "filled", "step0", "step1", "step2", "made0", "made1",
+               "made2", "vq0", "vq1", "xqd", "sent", "relay0", "relay1", "far_p", "diag", "plane", "mate_s", "mate_o", "mate_p",
+               "sib", "sib_p", "fwd_p", "fwd_d", "fwd_c", "st_a", "st_b", "st_c", "st_d", "st_e", "st_f", "st_g"]
               + ["mm%d" % s for s in range(N)] + ["cp%d" % s for s in range(N)])
 
 
@@ -39,46 +43,103 @@ def _roles(core, T, topo):
     return out
 
 
+def _same_die(a, b, topo):
+    return topo.host(a) == topo.host(b) and topo.chip(a) == topo.chip(b) and topo.die(a) == topo.die(b)
+
+
+def _relay(rank_core, mate, T, topo):
+    for c in range(WORLD):
+        if c not in T.cores and _same_die(c, rank_core, topo) and topo.may_write(c, mate):
+            return c
+
+
 def rank_program(g, core, T, topo):
-    rank = T.rank_of(core)
-    if rank is None:
-        return
     S = T.sem
+
+    def codes(s):
+        return T.codes[:, AT[s]:AT[s] + NC]
+
+    def planes(s, last=None):
+        return T.planes[:, AT[s]:AT[s if last is None else last] + NC]
+
+    def raw(s, a=0, b=NC):
+        return T.codes[:, AT[s] + a:AT[s] + b].bitcast(dt.uint8)
+
+    def first(s):
+        return raw(s, 0, EC)
+
+    def rest(s):
+        return raw(s, EC)
+
+    def to(d):
+        rid, pid = topo.addr(d, core)
+        return DstId(rid=rid, pnc=pid)
+
+    def move(view, dsts, mask, sem):
+        return RemoteDMATransfer(dst_ids=[to(c) for c, _ in dsts], dma_engine_mask=mask, remote_sem=sem,
+                                 srcs=[view(OWN)], dsts=[view(s) for _, s in dsts])
+
+    if T.rank_of(core) is None:
+        for r in T.cores:
+            if not _same_die(r, core, topo):
+                continue
+            role = _roles(r, T, topo)
+            mate = role[MATE_O]
+            if core != _relay(r, mate, T, topo):
+                continue
+            off = topo.mask(core, mate)
+            on = topo.mask(r, core) & ~topo.mask(r, mate)
+            e_off, e_on = bin(off).count("1"), bin(on).count("1")
+            for k, part in enumerate((first, rest)):
+                g.wait_ge(S["relay%d" % k], e_on)
+                g.remote_dma_fused([move(part, [(mate, MATE_O)], off, S.mate_o)], local_sem=S.sent)
+            g.wait_ge(S.sent, 2 * e_off)
+        return
+
     role = _roles(core, T, topo)
     sib = role[SIB]
     sib_role = _roles(sib, T, topo)
+    relay = _relay(core, role[MATE_O], T, topo)
     owner = dict(role)
     owner[SIB_PLANE] = sib_role[PLANE]
     owner[SIB_DIAG] = sib_role[DIAG]
 
-    def codes(s):
-        return T.codes[:, NC * s:NC * (s + 1)]
+    mid = (EC + NC) // 2
+    cut = (0, 4 * EC, 4 * mid, 4 * NC)
+    pad = 4 * AT[OWN]
+    g.sync.dma_start(T.gb[:, 0:cut[1]], T.gr[:, 0:cut[1]]).then_inc(S.ld_g0, 16)
+    g.sync.dma_start(T.gb[:, cut[1]:cut[3]], T.gr[:, cut[1]:cut[3]]).then_inc(S.ld_g1, 16)
+    for h in range(3):
+        g.scalar.dma_start(T.wb[:, cut[h]:cut[h + 1]], T.w[:, cut[h]:cut[h + 1]]).then_inc(S["ld_w%d" % h], 16)
+    g.scalar.dma_start(T.xb[:], T.x[:]).then_inc(S.ld_x, 16)
 
-    def planes(s, k=1):
-        return T.planes[:, NC * s:NC * (s + k)]
+    g.scalar.wait_ge(S.ld_g1, 16)
+    g.scalar.activation(T.step[:, cut[2]:cut[3]], T.gb[:, cut[2]:cut[3]], ActivationFunctionType.Copy, scale=0.125).then_inc(S.step2, 1)
 
-    def raw(s):
-        return codes(s).bitcast(dt.uint8)
-
-    H = 2 * NC
-    g.sync.dma_start(T.gb[:], T.gr[:]).then_inc(S.ld_g, 16)
-    for h in range(2):
-        g.scalar.dma_start(T.wb[:, H * h:H * (h + 1)], T.w[:, H * h:H * (h + 1)]).then_inc(S["ld_w%d" % h], 16)
-    g.sync.wait_ge(S.ld_g, 16)
-    g.sync.dma_start(T.xb[:], T.x[:]).then_inc(S.ld_x, 16)
-
-    g.vector.wait_ge(S.ld_g, 16)
-    g.vector.tensor_scalar(T.step[:, 0:H], T.gb[:, 0:H], 0.125, None, AluOpType.mult).then_inc(S.stepped0, 1)
-    g.scalar.wait_ge(S.ld_g, 16)
-    g.scalar.activation(T.step[:, H:2 * H], T.gb[:, H:2 * H], ActivationFunctionType.Copy, scale=0.125).then_inc(S.stepped1, 1)
-    for h in range(2):
+    def made(h):
+        a, b = cut[h], cut[h + 1]
+        if h < 2:
+            g.vector.wait_ge(S["ld_g%d" % h], 16)
+            g.vector.tensor_scalar(T.step[:, a:b], T.gb[:, a:b], 0.125, None, AluOpType.mult).then_inc(S["step%d" % h], 1)
+        g.vector.wait_ge(S["step%d" % h], 1)
         g.vector.wait_ge(S["ld_w%d" % h], 16)
-        g.vector.wait_ge(S["stepped%d" % h], 1)
-        half = slice(H * h, H * (h + 1))
-        g.vector.tensor_tensor(T.vb[:, half], T.wb[:, half], T.step[:, half], AluOpType.subtract).then_inc(S["made%d" % h], 1)
+        g.vector.tensor_tensor(T.vb[:, pad + a:pad + b], T.wb[:, a:b], T.step[:, a:b], AluOpType.subtract).then_inc(S["made%d" % h], 1)
+
+    def quantised(h):
+        g.vector.quantize_mx(T.codes[:, NC * h:NC * (h + 1)], T.planes[:, NC * h:NC * (h + 1)],
+                             T.vb[:, 4 * NC * h:4 * NC * (h + 1)]).then_inc(S["vq%d" % h], 1)
+
+    g.vector.memset(T.vb[:, 0:pad], 0.0).then_inc(S.filled, 1)
+    g.vector.memset(T.vb[:, pad + 4 * NC:8 * NC], 0.0).then_inc(S.filled, 1)
+    g.vector.wait_ge(S.filled, 2)
+    made(0)
     g.vector.wait_ge(S.made0, 1)
+    quantised(0)
+    made(1)
+    made(2)
     g.vector.wait_ge(S.made1, 1)
-    g.vector.quantize_mx(codes(OWN), planes(OWN), T.vb[:]).then_inc(S.vq, 1)
+    g.vector.wait_ge(S.made2, 1)
+    quantised(1)
     g.vector.wait_ge(S.ld_x, 16)
     g.vector.quantize_mx(T.xq[:], T.xs[:], T.xb[:]).then_inc(S.xqd, 1)
 
@@ -86,65 +147,63 @@ def rank_program(g, core, T, topo):
     on = topo.mask(core, sib) & ~off
     e_off, e_on = bin(off).count("1"), bin(on).count("1")
 
-    def to(d):
-        rid, pid = topo.addr(d, core)
-        return DstId(rid=rid, pnc=pid)
-
-    def own_to(view, roles, mask, sem):
-        return RemoteDMATransfer(dst_ids=[to(role[r]) for r in roles], dma_engine_mask=mask, remote_sem=sem,
-                                 srcs=[view(OWN)], dsts=[view(r) for r in roles])
+    def at(*roles):
+        return [(role[r], r) for r in roles]
 
     rid, pid = topo.addr(sib, core)
     mrid, mpid = topo.addr(role[MATE_S], core)
-    g.wait_ge(S.vq, 1)
-    g.remote_dma_fused([own_to(planes, (DIAG, PLANE), off, S.far_p)], local_sem=S.sent)
-    g.remote_dma_fused([own_to(raw, (DIAG,), off, S.diag)], local_sem=S.sent)
-    g.remote_dma(planes(SIB), planes(OWN), S.sib_p, S.sent, pid, rid, on)
-    g.remote_dma_fused([own_to(raw, (PLANE,), off, S.plane), own_to(raw, (SIB,), on, S.sib)], local_sem=S.sent)
-    g.remote_dma_fused([own_to(raw, (MATE_S, MATE_O), off, S.mate)], local_sem=S.sent)
+    g.wait_ge(S.vq0, 1)
+    g.remote_dma_fused([move(first, at(DIAG), off, S.diag), move(first, [(relay, OWN)], on, S.relay0)], local_sem=S.sent)
+    g.wait_ge(S.vq1, 1)
+    g.remote_dma_fused([move(planes, at(DIAG, PLANE), off, S.far_p), move(planes, at(SIB), on, S.sib_p)], local_sem=S.sent)
+    g.remote_dma_fused([move(rest, at(DIAG), off, S.diag), move(rest, [(relay, OWN)], on, S.relay1)], local_sem=S.sent)
+    g.remote_dma_fused([move(raw, at(PLANE), off, S.plane), move(raw, at(SIB), on, S.sib)], local_sem=S.sent)
+    g.remote_dma_fused([move(raw, at(MATE_S), off, S.mate_s)], local_sem=S.sent)
     g.wait_ge(S.sib_p, e_on)
-    g.remote_dma(planes(MATE_S, 2), planes(OWN, 2), S.mate_p, S.sent, mpid, mrid, off)
+    g.remote_dma(planes(MATE_S, MATE_O), planes(OWN, SIB), S.mate_p, S.sent, mpid, mrid, off)
     g.wait_ge(S.far_p, 2 * e_off)
-    g.remote_dma(planes(SIB_PLANE, 2), planes(PLANE, 2), S.fwd_p, S.sent, pid, rid, on)
-    g.wait_ge(S.diag, e_off)
-    g.remote_dma(raw(SIB_DIAG), raw(DIAG), S.fwd_d, S.sent, pid, rid, on)
+    g.remote_dma(planes(SIB_PLANE, SIB_DIAG), planes(PLANE, DIAG), S.fwd_p, S.sent, pid, rid, on)
+    g.wait_ge(S.diag, 2 * e_off)
+    g.remote_dma(raw(SIB_DIAG), raw(DIAG), S.fwd_d, S.sent, pid, rid, on | off)
     g.wait_ge(S.plane, e_off)
-    g.remote_dma(raw(SIB_PLANE), raw(PLANE), S.fwd_c, S.sent, pid, rid, on)
-    g.wait_ge(S.sent, 5 * e_off + 5 * e_on)
+    g.remote_dma(raw(SIB_PLANE), raw(PLANE), S.fwd_c, S.sent, pid, rid, on | off)
+    g.wait_ge(S.sent, 8 * e_off + 7 * e_on)
 
     def product(s):
         g.tensor.matmul_mx(T.ps[:, 512 * s:512 * s + NC], codes(s), planes(s), T.xq[:], T.xs[:], True, True).then_inc(S["mm%d" % s], 1)
 
-    g.tensor.wait_ge(S.vq, 1)
+    g.tensor.wait_ge(S.vq0, 1)
+    g.tensor.wait_ge(S.vq1, 1)
     g.tensor.wait_ge(S.xqd, 1)
     product(OWN)
     g.tensor.wait_ge(S.far_p, 2 * e_off)
-    g.tensor.wait_ge(S.diag, e_off)
+    g.tensor.wait_ge(S.diag, 2 * e_off)
     product(DIAG)
-    g.tensor.wait_ge(S.sib, e_on)
     g.tensor.wait_ge(S.sib_p, e_on)
+    g.tensor.wait_ge(S.sib, e_on)
     product(SIB)
     g.tensor.wait_ge(S.plane, e_off)
     product(PLANE)
-    g.tensor.wait_ge(S.fwd_p, e_on)
-    g.tensor.wait_ge(S.fwd_d, e_on)
-    product(SIB_DIAG)
     g.tensor.wait_ge(S.mate_p, e_off)
-    g.tensor.wait_ge(S.mate, 2 * e_off)
+    g.tensor.wait_ge(S.mate_s, e_off)
     product(MATE_S)
+    g.tensor.wait_ge(S.fwd_p, e_on)
+    g.tensor.wait_ge(S.fwd_d, e_on + e_off)
+    product(SIB_DIAG)
+    g.tensor.wait_ge(S.mate_o, 2 * e_off)
     product(MATE_O)
-    g.tensor.wait_ge(S.fwd_c, e_on)
+    g.tensor.wait_ge(S.fwd_c, e_on + e_off)
     product(SIB_PLANE)
 
     def block(s):
         j = T.rank_of(owner[s])
         return NC * j, NC * (j + 1)
 
-    for s in (OWN, SIB, SIB_DIAG, MATE_O):
+    for s in (DIAG, PLANE, SIB_DIAG):
         a, b = block(s)
         g.vector.wait_ge(S["mm%d" % s], 1)
         g.vector.tensor_copy(T.yb[:, a:b], T.ps[:, 512 * s:512 * s + NC]).then_inc(S["cp%d" % s], 1)
-    for s in (DIAG, PLANE, MATE_S, SIB_PLANE):
+    for s in (OWN, SIB, MATE_S, MATE_O, SIB_PLANE):
         a, b = block(s)
         g.scalar.wait_ge(S["mm%d" % s], 1)
         g.scalar.activation(T.yb[:, a:b], T.ps[:, 512 * s:512 * s + NC], ActivationFunctionType.Copy).then_inc(S["cp%d" % s], 1)
@@ -155,12 +214,13 @@ def rank_program(g, core, T, topo):
         a, b = min(block(s)[0] for s in slots), max(block(s)[1] for s in slots)
         q.dma_start(T.y[:, a:b], T.yb[:, a:b]).then_inc(sem, 16)
 
-    store(g.sync, (DIAG,), S.st_c)
     store(g.sync, (OWN, SIB), S.st_a)
     store(g.sync, (PLANE,), S.st_b)
+    store(g.sync, (DIAG,), S.st_c)
+    store(g.sync, (MATE_S,), S.st_d)
     store(g.sync, (SIB_DIAG,), S.st_e)
-    store(g.sync, (MATE_S, MATE_O), S.st_d)
-    store(g.scalar, (SIB_PLANE,), S.st_f)
-    for sem in (S.st_a, S.st_b, S.st_c, S.st_d, S.st_e):
+    store(g.sync, (MATE_O,), S.st_f)
+    store(g.scalar, (SIB_PLANE,), S.st_g)
+    for sem in (S.st_a, S.st_b, S.st_c, S.st_d, S.st_e, S.st_f):
         g.sync.wait_ge(sem, 16)
-    g.scalar.wait_ge(S.st_f, 16)
+    g.scalar.wait_ge(S.st_g, 16)

from concourse.bass import DstId, RemoteDMATransfer
from concourse.mybir import dt, AluOpType, ActivationFunctionType

N = 8
WORLD = 256
NC = 128
EC = 32
OWN, SIB, MATE_S, MATE_O, PLANE, DIAG, SIB_PLANE, SIB_DIAG = range(N)
AT = [NC - EC, 2 * NC, 3 * NC, 4 * NC + EC] + [EC + NC * k for k in range(5, 9)]
COLS = AT[SIB_DIAG] + NC

SCRATCH = {
    "wb": ("sbuf", [128, 4 * NC], "bfloat16"),
    "gb": ("sbuf", [128, 4 * NC], "bfloat16"),
    "xb": ("sbuf", [128, 4 * NC], "bfloat16"),
    "step": ("sbuf", [128, 4 * NC], "bfloat16"),
    "vb": ("sbuf", [128, 8 * NC], "bfloat16"),
    "codes": ("sbuf", [128, COLS], "float8_e4m3fn_x4"),
    "planes": ("sbuf", [128, COLS], "uint8"),
    "xq": ("sbuf", [128, NC], "float8_e4m3fn_x4"),
    "xs": ("sbuf", [128, NC], "uint8"),
    "ps": ("psum", [128, 512 * N], "float32"),
    "yb": ("sbuf", [128, N * NC], "float32"),
}
SEMAPHORES = (["ld_g0", "ld_g1", "ld_w0", "ld_w1", "ld_w2", "ld_x", "filled", "step0", "step1", "step2", "made0", "made1",
               "made2", "vq0", "vq1", "xqd", "sent", "relay0", "relay1", "far_p", "diag", "plane", "mate_s", "mate_o", "mate_p",
               "sib", "sib_p", "fwd_p", "fwd_d", "fwd_c", "st_a", "st_b", "st_c", "st_d", "st_e", "st_f", "st_g"]
              + ["mm%d" % s for s in range(N)] + ["cp%d" % s for s in range(N)])


def _roles(core, T, topo):
    out = {OWN: core}
    for c in T.cores:
        if c == core:
            continue
        near = topo.die(c) == topo.die(core)
        if topo.host(c) == topo.host(core) and topo.chip(c) == topo.chip(core):
            out[SIB] = c
        elif topo.mates(core, c):
            out[MATE_S if near else MATE_O] = c
        elif near:
            out[PLANE if topo.same_plane(core, c) else DIAG] = c
    return out


def _same_die(a, b, topo):
    return topo.host(a) == topo.host(b) and topo.chip(a) == topo.chip(b) and topo.die(a) == topo.die(b)


def _relay(rank_core, mate, T, topo):
    for c in range(WORLD):
        if c not in T.cores and _same_die(c, rank_core, topo) and topo.may_write(c, mate):
            return c


def rank_program(g, core, T, topo):
    S = T.sem

    def codes(s):
        return T.codes[:, AT[s]:AT[s] + NC]

    def planes(s, last=None):
        return T.planes[:, AT[s]:AT[s if last is None else last] + NC]

    def raw(s, a=0, b=NC):
        return T.codes[:, AT[s] + a:AT[s] + b].bitcast(dt.uint8)

    def first(s):
        return raw(s, 0, EC)

    def rest(s):
        return raw(s, EC)

    def to(d):
        rid, pid = topo.addr(d, core)
        return DstId(rid=rid, pnc=pid)

    def move(view, dsts, mask, sem):
        return RemoteDMATransfer(dst_ids=[to(c) for c, _ in dsts], dma_engine_mask=mask, remote_sem=sem,
                                 srcs=[view(OWN)], dsts=[view(s) for _, s in dsts])

    if T.rank_of(core) is None:
        for r in T.cores:
            if not _same_die(r, core, topo):
                continue
            role = _roles(r, T, topo)
            mate = role[MATE_O]
            if core != _relay(r, mate, T, topo):
                continue
            off = topo.mask(core, mate)
            on = topo.mask(r, core) & ~topo.mask(r, mate)
            e_off, e_on = bin(off).count("1"), bin(on).count("1")
            for k, part in enumerate((first, rest)):
                g.wait_ge(S["relay%d" % k], e_on)
                g.remote_dma_fused([move(part, [(mate, MATE_O)], off, S.mate_o)], local_sem=S.sent)
            g.wait_ge(S.sent, 2 * e_off)
        return

    role = _roles(core, T, topo)
    sib = role[SIB]
    sib_role = _roles(sib, T, topo)
    relay = _relay(core, role[MATE_O], T, topo)
    owner = dict(role)
    owner[SIB_PLANE] = sib_role[PLANE]
    owner[SIB_DIAG] = sib_role[DIAG]

    mid = (EC + NC) // 2
    cut = (0, 4 * EC, 4 * mid, 4 * NC)
    pad = 4 * AT[OWN]
    g.sync.dma_start(T.gb[:, 0:cut[1]], T.gr[:, 0:cut[1]]).then_inc(S.ld_g0, 16)
    g.sync.dma_start(T.gb[:, cut[1]:cut[3]], T.gr[:, cut[1]:cut[3]]).then_inc(S.ld_g1, 16)
    for h in range(3):
        g.scalar.dma_start(T.wb[:, cut[h]:cut[h + 1]], T.w[:, cut[h]:cut[h + 1]]).then_inc(S["ld_w%d" % h], 16)
    g.scalar.dma_start(T.xb[:], T.x[:]).then_inc(S.ld_x, 16)

    g.scalar.wait_ge(S.ld_g1, 16)
    g.scalar.activation(T.step[:, cut[2]:cut[3]], T.gb[:, cut[2]:cut[3]], ActivationFunctionType.Copy, scale=0.125).then_inc(S.step2, 1)

    def made(h):
        a, b = cut[h], cut[h + 1]
        if h < 2:
            g.vector.wait_ge(S["ld_g%d" % h], 16)
            g.vector.tensor_scalar(T.step[:, a:b], T.gb[:, a:b], 0.125, None, AluOpType.mult).then_inc(S["step%d" % h], 1)
        g.vector.wait_ge(S["step%d" % h], 1)
        g.vector.wait_ge(S["ld_w%d" % h], 16)
        g.vector.tensor_tensor(T.vb[:, pad + a:pad + b], T.wb[:, a:b], T.step[:, a:b], AluOpType.subtract).then_inc(S["made%d" % h], 1)

    def quantised(h):
        g.vector.quantize_mx(T.codes[:, NC * h:NC * (h + 1)], T.planes[:, NC * h:NC * (h + 1)],
                             T.vb[:, 4 * NC * h:4 * NC * (h + 1)]).then_inc(S["vq%d" % h], 1)

    g.vector.memset(T.vb[:, 0:pad], 0.0).then_inc(S.filled, 1)
    g.vector.memset(T.vb[:, pad + 4 * NC:8 * NC], 0.0).then_inc(S.filled, 1)
    g.vector.wait_ge(S.filled, 2)
    made(0)
    g.vector.wait_ge(S.made0, 1)
    quantised(0)
    made(1)
    made(2)
    g.vector.wait_ge(S.made1, 1)
    g.vector.wait_ge(S.made2, 1)
    quantised(1)
    g.vector.wait_ge(S.ld_x, 16)
    g.vector.quantize_mx(T.xq[:], T.xs[:], T.xb[:]).then_inc(S.xqd, 1)

    off = topo.mask(core, role[PLANE])
    on = topo.mask(core, sib) & ~off
    e_off, e_on = bin(off).count("1"), bin(on).count("1")

    def at(*roles):
        return [(role[r], r) for r in roles]

    rid, pid = topo.addr(sib, core)
    mrid, mpid = topo.addr(role[MATE_S], core)
    g.wait_ge(S.vq0, 1)
    g.remote_dma_fused([move(first, at(DIAG), off, S.diag), move(first, [(relay, OWN)], on, S.relay0)], local_sem=S.sent)
    g.wait_ge(S.vq1, 1)
    g.remote_dma_fused([move(planes, at(DIAG, PLANE), off, S.far_p), move(planes, at(SIB), on, S.sib_p)], local_sem=S.sent)
    g.remote_dma_fused([move(rest, at(DIAG), off, S.diag), move(rest, [(relay, OWN)], on, S.relay1)], local_sem=S.sent)
    g.remote_dma_fused([move(raw, at(PLANE), off, S.plane), move(raw, at(SIB), on, S.sib)], local_sem=S.sent)
    g.remote_dma_fused([move(raw, at(MATE_S), off, S.mate_s)], local_sem=S.sent)
    g.wait_ge(S.sib_p, e_on)
    g.remote_dma(planes(MATE_S, MATE_O), planes(OWN, SIB), S.mate_p, S.sent, mpid, mrid, off)
    g.wait_ge(S.far_p, 2 * e_off)
    g.remote_dma(planes(SIB_PLANE, SIB_DIAG), planes(PLANE, DIAG), S.fwd_p, S.sent, pid, rid, on)
    g.wait_ge(S.diag, 2 * e_off)
    g.remote_dma(raw(SIB_DIAG), raw(DIAG), S.fwd_d, S.sent, pid, rid, on | off)
    g.wait_ge(S.plane, e_off)
    g.remote_dma(raw(SIB_PLANE), raw(PLANE), S.fwd_c, S.sent, pid, rid, on | off)
    g.wait_ge(S.sent, 8 * e_off + 7 * e_on)

    def product(s):
        g.tensor.matmul_mx(T.ps[:, 512 * s:512 * s + NC], codes(s), planes(s), T.xq[:], T.xs[:], True, True).then_inc(S["mm%d" % s], 1)

    g.tensor.wait_ge(S.vq0, 1)
    g.tensor.wait_ge(S.vq1, 1)
    g.tensor.wait_ge(S.xqd, 1)
    product(OWN)
    g.tensor.wait_ge(S.far_p, 2 * e_off)
    g.tensor.wait_ge(S.diag, 2 * e_off)
    product(DIAG)
    g.tensor.wait_ge(S.sib_p, e_on)
    g.tensor.wait_ge(S.sib, e_on)
    product(SIB)
    g.tensor.wait_ge(S.plane, e_off)
    product(PLANE)
    g.tensor.wait_ge(S.mate_p, e_off)
    g.tensor.wait_ge(S.mate_s, e_off)
    product(MATE_S)
    g.tensor.wait_ge(S.fwd_p, e_on)
    g.tensor.wait_ge(S.fwd_d, e_on + e_off)
    product(SIB_DIAG)
    g.tensor.wait_ge(S.mate_o, 2 * e_off)
    product(MATE_O)
    g.tensor.wait_ge(S.fwd_c, e_on + e_off)
    product(SIB_PLANE)

    def block(s):
        j = T.rank_of(owner[s])
        return NC * j, NC * (j + 1)

    for s in (DIAG, PLANE, SIB_DIAG):
        a, b = block(s)
        g.vector.wait_ge(S["mm%d" % s], 1)
        g.vector.tensor_copy(T.yb[:, a:b], T.ps[:, 512 * s:512 * s + NC]).then_inc(S["cp%d" % s], 1)
    for s in (OWN, SIB, MATE_S, MATE_O, SIB_PLANE):
        a, b = block(s)
        g.scalar.wait_ge(S["mm%d" % s], 1)
        g.scalar.activation(T.yb[:, a:b], T.ps[:, 512 * s:512 * s + NC], ActivationFunctionType.Copy).then_inc(S["cp%d" % s], 1)

    def store(q, slots, sem):
        for s in slots:
            q.wait_ge(S["cp%d" % s], 1)
        a, b = min(block(s)[0] for s in slots), max(block(s)[1] for s in slots)
        q.dma_start(T.y[:, a:b], T.yb[:, a:b]).then_inc(sem, 16)

    store(g.sync, (OWN, SIB), S.st_a)
    store(g.sync, (PLANE,), S.st_b)
    store(g.sync, (DIAG,), S.st_c)
    store(g.sync, (MATE_S,), S.st_d)
    store(g.sync, (SIB_DIAG,), S.st_e)
    store(g.sync, (MATE_O,), S.st_f)
    store(g.scalar, (SIB_PLANE,), S.st_g)
    for sem in (S.st_a, S.st_b, S.st_c, S.st_d, S.st_e, S.st_f):
        g.sync.wait_ge(sem, 16)
    g.scalar.wait_ge(S.st_g, 16)
